import numpy as np
import ml_dtypes


def mxq(x, axis, fmt="e4m3"):
    dtype, down = {"e4m3": (ml_dtypes.float8_e4m3fn, 7), "e5m2": (ml_dtypes.float8_e5m2, 14)}[fmt]
    v = np.moveaxis(np.asarray(x, np.float32).astype(ml_dtypes.bfloat16).astype(np.float64), axis, -1)
    blocks = v.reshape(v.shape[:-1] + (-1, 32))
    amax = np.abs(blocks).max(-1, keepdims=True)
    byte = np.maximum(np.where(amax > 0, np.frexp(amax)[1] - 1 + 127, 0) - down, 1)
    scale = np.exp2(byte - 127.0)
    codes = (blocks / scale).astype(np.float32).astype(dtype).astype(np.float64)
    return np.moveaxis((codes * scale).reshape(v.shape), -1, axis)


WIDE = False


def mx_kscale(k):
    if not WIDE:
        return np.ones(k)
    levels = np.array([10, -10, 5, -5, 0])
    if k % 512:
        return np.exp2(np.random.permutation(np.resize(levels, k // 32))).repeat(32)
    a = np.empty((k // 512, 16))
    for p in range(k // 512):
        a[p, :8] = np.random.permutation(np.resize(levels, 8))
        for g in range(8):
            far = levels[np.abs(levels - a[p, g]) >= 10]
            a[p, g + 8] = far[np.random.randint(len(far))]
    return np.exp2(a.ravel()).repeat(32)


def f64(x):
    return np.asarray(x).astype(np.float64)


def striped(idx):
    return np.tile(np.asarray(idx).reshape(-1, 16).T, (8, 1)).astype(np.uint16)


def unstriped(offs):
    return offs[:16].T.reshape(-1).astype(np.int64)


B, N, T, D, DV, NQ = 1, 1024, 4096, 512, 256, 128


def setup_inputs():
    n = np.random.standard_normal
    idx = np.sort(np.random.permutation(T)[:B * N].reshape(B, N), axis=1).reshape(-1)
    s = mx_kscale(D)[:, None]
    u = np.ones(T)
    u[idx] = mx_kscale(B * N)
    r = np.random.uniform(0.5, 2.0, T)
    rk = np.random.uniform(0.5, 2.0, T)
    k = n((D, T)) / s / rk
    v = n((DV, T)) / (u * r)
    return {
        "qT": (n((B, D, NQ)) * s * (1.00 / np.sqrt(D))).astype(np.float32),
        "kT": k.astype(np.float32),
        "vT": v.astype(np.float32),
        "ks": np.tile(rk, (128, 1)).astype(np.float32),
        "vs": np.tile(u * r, (128, 1)).astype(np.float32),
        "kb": np.tile(n(T), (128, 1)).astype(np.float32),
        "offs": striped(idx),
    }


def reference(qT, kT, vT, ks, vs, kb, offs):
    idx = unstriped(offs)
    k = f64(kT)
    v = f64(vT)
    pick = lambda x: x[:, idx].reshape(x.shape[0], B, N).transpose(1, 0, 2)
    q = f64(qT)
    score = mxq(q, 1, "e4m3").transpose(0, 2, 1) @ mxq(pick(k), 1, "e4m3")
    score = score * pick(f64(ks))[:, :1, :]
    score = score + pick(f64(kb))[:, :1, :]
    p = 1.0 / (1.0 + np.exp(-score))
    w = p * pick(f64(vs))[:, :1, :]
    y = mxq(w, 2, "e4m3") @ mxq(pick(v).transpose(0, 2, 1), 1, "e4m3")
    y = y / 16.0
    return y

@@ -1,0 +1,183 @@
+from contextlib import ExitStack
+
+import concourse.mybir as mybir
+from concourse.masks import make_identity
+
+F32 = mybir.dt.float32
+BF16 = mybir.dt.bfloat16
+U32 = mybir.dt.uint32
+U16 = mybir.dt.uint16
+U8 = mybir.dt.uint8
+FP8X4 = mybir.dt.float8_e4m3fn_x4
+ACT = mybir.ActivationFunctionType
+MULT = mybir.AluOpType.mult
+
+P = 128
+T = 4096
+N = 1024
+D = 512
+DV = 256
+NQ = 128
+HALF = 512
+FLOPS = 2 * N * NQ * (D + DV)
+BYTES = 4 * (D * T + DV * T + D * NQ + 3 * T + NQ * DV) + 2 * P * N // 16
+
+
+def tile_attend_sigmoid_ks_srt_kernel(tc, qT, kT, vT, ks, vs, kb, offs, out):
+    nc = tc.nc
+    with ExitStack() as ctx:
+        held = ctx.enter_context(tc.tile_pool(name="held", bufs=1))
+        psum_t = ctx.enter_context(tc.psum_pool(name="psum_t", bufs=4))
+        psum_s = ctx.enter_context(tc.psum_pool(name="psum_s", bufs=1))
+
+        offsets = held.tile([P, N // 16], U16, name="offsets")
+        nc.sync.dma_start(offsets[:], offs)
+
+        rows = {}
+        gathered_rows = {}
+        columns = {}
+        for name in ("ks", "kb", "vs"):
+            rows[name] = held.tile([P, T], F32, name="row_" + name)
+            gathered_rows[name] = held.tile([P, N], F32, name="picked_" + name)
+            columns[name] = held.tile([P, 2, 4], F32, name="col_" + name)
+        k_pool = [held.tile([P, T], F32, name="k_pool_%d" % t) for t in range(4)]
+        v_pool = [held.tile([P, T], F32, name="v_pool_%d" % c) for c in range(2)]
+        k_rows = kT.rearrange("(p j) w -> p j w", j=4)
+        q_raw = held.tile([P, 4, NQ], F32, name="q_raw")
+        warm = held.tile([P, 1], F32, name="warm")
+        ident = held.tile([P, P], F32, name="ident")
+
+        nc.sync.dma_start(out=k_pool[0][:], in_=k_rows[:, 0, :])
+        nc.sync.dma_start(out=q_raw[:], in_=qT[0].rearrange("(p j) q -> p j q", j=4))
+        nc.vector.memset(warm[:], 0.0)
+        nc.scalar.activation(out=warm[:], in_=warm[:], func=ACT.Sigmoid)
+        nc.gpsimd.memset(rows["ks"][:], 0.0)
+        nc.scalar.dma_start(out=rows["ks"][0:1, :], in_=ks[0:1, :])
+        nc.gpsimd.memset(k_pool[1][:, 0:8], 0.0)
+        nc.sync.dma_start(out=k_pool[1][:], in_=k_rows[:, 1, :])
+        nc.gpsimd.memset(rows["kb"][:], 0.0)
+        nc.scalar.dma_start(out=rows["kb"][0:1, :], in_=kb[0:1, :])
+        nc.gpsimd.memset(k_pool[2][:, 0:8], 0.0)
+        nc.sync.dma_start(out=k_pool[2][:], in_=k_rows[:, 2, :])
+        make_identity(nc, ident[:])
+        nc.gpsimd.memset(rows["vs"][:], 0.0)
+        nc.scalar.dma_start(out=rows["vs"][0:1, :], in_=vs[0:1, :])
+        for late in (k_pool[3], v_pool[0], v_pool[1]):
+            nc.gpsimd.memset(late[:, 0:8], 0.0)
+        nc.sync.dma_start(out=k_pool[3][:], in_=k_rows[:, 3, :])
+        nc.sync.dma_start(out=v_pool[0][:], in_=vT[0:P, :])
+        nc.sync.dma_start(out=v_pool[1][:], in_=vT[P : 2 * P, :])
+
+        gk = held.tile([P, 4, N], F32, name="gk")
+        gv = [held.tile([P, N], F32, name="gv_%d" % c) for c in range(2)]
+        k_grouped = [held.tile([P, 4, P, 4], BF16, name="k_grouped_%d" % h, align_bytes=64) for h in range(2)]
+        k_codes = [held.tile([P, HALF], U32, name="k_codes_%d" % h, align_bytes=64) for h in range(2)]
+        k_scales = [held.tile([P, HALF], U8, name="k_scales_%d" % h, align_bytes=64) for h in range(2)]
+        q_grouped = held.tile([P, NQ, 4], BF16, name="q_grouped", align_bytes=64)
+        q_codes = held.tile([P, NQ], U32, name="q_codes", align_bytes=64)
+        q_scales = held.tile([P, NQ], U8, name="q_scales", align_bytes=64)
+
+        def gather_row(name):
+            nc.vector.tensor_copy(gathered_rows[name][:], rows[name][:].indirect(offsets[:]))
+
+        def turn_row(name):
+            for h in range(2):
+                bank = psum_t.tile([P, 4, P], F32, name="turned")
+                for t in range(4):
+                    nc.tensor.transpose(bank[:, t, :], gathered_rows[name][:, HALF * h + t : HALF * (h + 1) : 4], ident[:])
+                nc.scalar.copy(out=columns[name][:, h, :], in_=bank[:, :, 0])
+
+        def gather_k(t, h0, h1):
+            nc.vector.tensor_copy(
+                gk[:, t, HALF * h0 : HALF * h1], k_pool[t][:].indirect(offsets[:, 32 * h0 : 32 * h1])
+            )
+
+        def group_k(pair, h):
+            nc.scalar.copy(
+                out=k_grouped[h][:, :, :, 2 * pair : 2 * pair + 2].rearrange("p t s d -> p s t d"),
+                in_=gk[:, 2 * pair : 2 * pair + 2, HALF * h : HALF * (h + 1)].rearrange("p d (s t) -> p s t d", t=4),
+            )
+
+        def quantise(codes, scales, values):
+            nc.vector.quantize_mx(out=codes.bitcast(FP8X4), scales=scales, in_=values)
+
+        gather_row("ks")
+        gather_k(0, 0, 2)
+        turn_row("ks")
+        gather_row("kb")
+        nc.scalar.copy(out=q_grouped[:], in_=q_raw[:].rearrange("p j q -> p q j"))
+        gather_k(1, 0, 2)
+        turn_row("kb")
+        quantise(q_codes[:], q_scales[:], q_grouped[:].rearrange("p q j -> p (q j)"))
+        group_k(0, 0)
+        group_k(0, 1)
+        gather_k(2, 0, 2)
+        gather_row("vs")
+        turn_row("vs")
+        w_codes = []
+        w_scales = []
+        for h in range(2):
+            gather_k(3, h, h + 1)
+            group_k(1, h)
+        for h in range(2):
+            quantise(k_codes[h][:], k_scales[h][:], k_grouped[h][:].rearrange("p t s d -> p (t s d)"))
+            scores = psum_s.tile([P, 4, NQ], F32, name="scores_%d" % h)
+            for t in range(4):
+                nc.tensor.matmul_mx(
+                    out=scores[:, t, :],
+                    lhsT=k_codes[h][:, P * t : P * (t + 1)].bitcast(FP8X4),
+                    lhsT_scale=k_scales[h][:, P * t : P * (t + 1)],
+                    rhs=q_codes[:].bitcast(FP8X4),
+                    rhs_scale=q_scales[:],
+                    start=True,
+                    stop=True,
+                )
+            probs = held.tile([P, 4, NQ], F32, name="probs_%d" % h)
+            for t in range(4):
+                nc.scalar.activation(
+                    out=probs[:, t, :],
+                    in_=scores[:, t, :],
+                    func=ACT.Sigmoid,
+                    bias=columns["kb"][:, h, t : t + 1],
+                    scale=columns["ks"][:, h, t : t + 1],
+                )
+            w_grouped = held.tile([P, NQ, 4], BF16, name="w_grouped_%d" % h, align_bytes=64)
+            nc.vector.tensor_tensor(
+                w_grouped[:],
+                probs[:].rearrange("p t q -> p q t"),
+                columns["vs"][:, h, :].unsqueeze(1).to_broadcast([P, NQ, 4]),
+                MULT,
+            )
+            codes = held.tile([P, NQ], U32, name="w_codes_%d" % h, align_bytes=64)
+            scales = held.tile([P, NQ], U8, name="w_scales_%d" % h, align_bytes=64)
+            quantise(codes[:], scales[:], w_grouped[:].rearrange("p q t -> p (q t)"))
+            w_codes.append(codes)
+            w_scales.append(scales)
+
+        for c in range(2):
+            acc = psum_s.tile([P, P], F32, name="acc_%d" % c)
+            for h in range(2):
+                nc.vector.tensor_copy(
+                    gv[c][:, HALF * h : HALF * (h + 1)], v_pool[c][:].indirect(offsets[:, 32 * h : 32 * (h + 1)])
+                )
+            for h in range(2):
+                bank = psum_t.tile([P, 4, P], F32, name="turned")
+                for t in range(4):
+                    nc.tensor.transpose(bank[:, t, :], gv[c][:, HALF * h + t : HALF * (h + 1) : 4], ident[:])
+                v_grouped = held.tile([P, P, 4], BF16, name="v_grouped_%d_%d" % (c, h), align_bytes=64)
+                nc.scalar.copy(out=v_grouped[:], in_=bank[:].rearrange("p t e -> p e t"))
+                codes = held.tile([P, P], U32, name="v_codes_%d_%d" % (c, h), align_bytes=64)
+                scales = held.tile([P, P], U8, name="v_scales_%d_%d" % (c, h), align_bytes=64)
+                quantise(codes[:], scales[:], v_grouped[:].rearrange("p e t -> p (e t)"))
+                nc.tensor.matmul_mx(
+                    out=acc[:],
+                    lhsT=w_codes[h][:].bitcast(FP8X4),
+                    lhsT_scale=w_scales[h][:],
+                    rhs=codes[:].bitcast(FP8X4),
+                    rhs_scale=scales[:],
+                    start=(h == 0),
+                    stop=(h == 1),
+                )
+            result = held.tile([P, P], F32, name="result_%d" % c)
+            nc.scalar.activation(out=result[:], in_=acc[:], func=ACT.Copy, scale=1.0 / 16.0)
+            nc.sync.dma_start(out=out[0, :, P * c : P * (c + 1)], in_=result[:])

@@ -49,28 +49,27 @@ def tile_attend_sigmoid_ks_srt_kernel(tc, qT, kT, vT, ks, vs, kb, offs, out):
 
         nc.sync.dma_start(out=k_pool[0][:], in_=k_rows[:, 0, :])
         nc.sync.dma_start(out=q_raw[:], in_=qT[0].rearrange("(p j) q -> p j q", j=4))
+        make_identity(nc, ident[:])
+        nc.vector.memset(rows["ks"][:], 0.0)
+        nc.sync.dma_start(out=rows["ks"][0:1, :], in_=ks[0:1, :])
+        nc.vector.memset(rows["kb"][:], 0.0)
+        nc.sync.dma_start(out=rows["kb"][0:1, :], in_=kb[0:1, :])
+        nc.vector.memset(k_pool[1][:, 0:8], 0.0)
+        nc.sync.dma_start(out=k_pool[1][:], in_=k_rows[:, 1, :])
+        nc.vector.memset(rows["vs"][:], 0.0)
+        nc.sync.dma_start(out=rows["vs"][0:1, :], in_=vs[0:1, :])
         nc.vector.memset(warm[:], 0.0)
         nc.scalar.activation(out=warm[:], in_=warm[:], func=ACT.Sigmoid)
-        nc.gpsimd.memset(rows["ks"][:], 0.0)
-        nc.scalar.dma_start(out=rows["ks"][0:1, :], in_=ks[0:1, :])
-        nc.gpsimd.memset(k_pool[1][:, 0:8], 0.0)
-        nc.sync.dma_start(out=k_pool[1][:], in_=k_rows[:, 1, :])
-        nc.gpsimd.memset(rows["kb"][:], 0.0)
-        nc.scalar.dma_start(out=rows["kb"][0:1, :], in_=kb[0:1, :])
-        nc.gpsimd.memset(k_pool[2][:, 0:8], 0.0)
-        nc.sync.dma_start(out=k_pool[2][:], in_=k_rows[:, 2, :])
-        make_identity(nc, ident[:])
-        nc.gpsimd.memset(rows["vs"][:], 0.0)
-        nc.scalar.dma_start(out=rows["vs"][0:1, :], in_=vs[0:1, :])
-        for late in (k_pool[3], v_pool[0], v_pool[1]):
-            nc.gpsimd.memset(late[:, 0:8], 0.0)
-        nc.sync.dma_start(out=k_pool[3][:], in_=k_rows[:, 3, :])
-        nc.sync.dma_start(out=v_pool[0][:], in_=vT[0:P, :])
-        nc.sync.dma_start(out=v_pool[1][:], in_=vT[P : 2 * P, :])
+        for late in (k_pool[2], k_pool[3], v_pool[0], v_pool[1]):
+            nc.vector.memset(late[:, 0:8], 0.0)
+        for t in range(2, 4):
+            nc.sync.dma_start(out=k_pool[t][:], in_=k_rows[:, t, :])
+        for c in range(2):
+            nc.sync.dma_start(out=v_pool[c][:], in_=vT[P * c : P * (c + 1), :])
 
         gk = held.tile([P, 4, N], F32, name="gk")
-        gv = [held.tile([P, N], F32, name="gv_%d" % c) for c in range(2)]
-        k_grouped = [held.tile([P, 4, P, 4], BF16, name="k_grouped_%d" % h, align_bytes=64) for h in range(2)]
+        gv = {}
+        k_grouped = [held.tile([P, 4, P, 4], BF16, name="k_grouped_%d" % h, tag="k_grouped_%d" % h, align_bytes=64) for h in range(2)]
         k_codes = [held.tile([P, HALF], U32, name="k_codes_%d" % h, align_bytes=64) for h in range(2)]
         k_scales = [held.tile([P, HALF], U8, name="k_scales_%d" % h, align_bytes=64) for h in range(2)]
         q_grouped = held.tile([P, NQ, 4], BF16, name="q_grouped", align_bytes=64)
@@ -80,12 +79,18 @@ def tile_attend_sigmoid_ks_srt_kernel(tc, qT, kT, vT, ks, vs, kb, offs, out):
         def gather_row(name):
             nc.vector.tensor_copy(gathered_rows[name][:], rows[name][:].indirect(offsets[:]))
 
+        def turn(source):
+            bank = psum_t.tile([P, 4, P], F32, name="turned")
+            for t in range(4):
+                nc.tensor.transpose(bank[:, t, :], source[:, t:HALF:4], ident[:])
+            return bank
+
         def turn_row(name):
+            return [turn(gathered_rows[name][:, HALF * h : HALF * (h + 1)]) for h in range(2)]
+
+        def keep_columns(name, banks):
             for h in range(2):
-                bank = psum_t.tile([P, 4, P], F32, name="turned")
-                for t in range(4):
-                    nc.tensor.transpose(bank[:, t, :], gathered_rows[name][:, HALF * h + t : HALF * (h + 1) : 4], ident[:])
-                nc.scalar.copy(out=columns[name][:, h, :], in_=bank[:, :, 0])
+                nc.scalar.copy(out=columns[name][:, h, :], in_=banks[h][:, :, 0])
 
         def gather_k(t, h0, h1):
             nc.vector.tensor_copy(
@@ -101,30 +106,11 @@ def tile_attend_sigmoid_ks_srt_kernel(tc, qT, kT, vT, ks, vs, kb, offs, out):
         def quantise(codes, scales, values):
             nc.vector.quantize_mx(out=codes.bitcast(FP8X4), scales=scales, in_=values)
 
-        gather_row("ks")
-        gather_k(0, 0, 2)
-        turn_row("ks")
-        gather_row("kb")
-        nc.scalar.copy(out=q_grouped[:], in_=q_raw[:].rearrange("p j q -> p q j"))
-        gather_k(1, 0, 2)
-        turn_row("kb")
-        quantise(q_codes[:], q_scales[:], q_grouped[:].rearrange("p q j -> p (q j)"))
-        group_k(0, 0)
-        group_k(0, 1)
-        gather_k(2, 0, 2)
-        gather_row("vs")
-        turn_row("vs")
-        w_codes = []
-        w_scales = []
-        for h in range(2):
-            gather_k(3, h, h + 1)
-            group_k(1, h)
-        for h in range(2):
+        def score(h):
             quantise(k_codes[h][:], k_scales[h][:], k_grouped[h][:].rearrange("p t s d -> p (t s d)"))
-            scores = psum_s.tile([P, 4, NQ], F32, name="scores_%d" % h)
             for t in range(4):
                 nc.tensor.matmul_mx(
-                    out=scores[:, t, :],
+                    out=scores[h][:, t, :],
                     lhsT=k_codes[h][:, P * t : P * (t + 1)].bitcast(FP8X4),
                     lhsT_scale=k_scales[h][:, P * t : P * (t + 1)],
                     rhs=q_codes[:].bitcast(FP8X4),
@@ -132,52 +118,102 @@ def tile_attend_sigmoid_ks_srt_kernel(tc, qT, kT, vT, ks, vs, kb, offs, out):
                     start=True,
                     stop=True,
                 )
-            probs = held.tile([P, 4, NQ], F32, name="probs_%d" % h)
+
+        def squash(h):
             for t in range(4):
                 nc.scalar.activation(
-                    out=probs[:, t, :],
-                    in_=scores[:, t, :],
+                    out=probs[h][:, t, :],
+                    in_=scores[h][:, t, :],
                     func=ACT.Sigmoid,
                     bias=columns["kb"][:, h, t : t + 1],
                     scale=columns["ks"][:, h, t : t + 1],
                 )
-            w_grouped = held.tile([P, NQ, 4], BF16, name="w_grouped_%d" % h, align_bytes=64)
+
+        def weigh(h):
             nc.vector.tensor_tensor(
-                w_grouped[:],
-                probs[:].rearrange("p t q -> p q t"),
+                w_grouped[h][:],
+                probs[h][:].rearrange("p t q -> p q t"),
                 columns["vs"][:, h, :].unsqueeze(1).to_broadcast([P, NQ, 4]),
                 MULT,
             )
-            codes = held.tile([P, NQ], U32, name="w_codes_%d" % h, align_bytes=64)
-            scales = held.tile([P, NQ], U8, name="w_scales_%d" % h, align_bytes=64)
-            quantise(codes[:], scales[:], w_grouped[:].rearrange("p q t -> p (q t)"))
-            w_codes.append(codes)
-            w_scales.append(scales)
+            quantise(w_codes[h][:], w_scales[h][:], w_grouped[h][:].rearrange("p q t -> p (q t)"))
 
-        for c in range(2):
-            acc = psum_s.tile([P, P], F32, name="acc_%d" % c)
-            for h in range(2):
-                nc.vector.tensor_copy(
-                    gv[c][:, HALF * h : HALF * (h + 1)], v_pool[c][:].indirect(offsets[:, 32 * h : 32 * (h + 1)])
-                )
-            for h in range(2):
-                bank = psum_t.tile([P, 4, P], F32, name="turned")
-                for t in range(4):
-                    nc.tensor.transpose(bank[:, t, :], gv[c][:, HALF * h + t : HALF * (h + 1) : 4], ident[:])
-                v_grouped = held.tile([P, P, 4], BF16, name="v_grouped_%d_%d" % (c, h), align_bytes=64)
-                nc.scalar.copy(out=v_grouped[:], in_=bank[:].rearrange("p t e -> p e t"))
-                codes = held.tile([P, P], U32, name="v_codes_%d_%d" % (c, h), align_bytes=64)
-                scales = held.tile([P, P], U8, name="v_scales_%d_%d" % (c, h), align_bytes=64)
-                quantise(codes[:], scales[:], v_grouped[:].rearrange("p e t -> p (e t)"))
-                nc.tensor.matmul_mx(
-                    out=acc[:],
-                    lhsT=w_codes[h][:].bitcast(FP8X4),
-                    lhsT_scale=w_scales[h][:],
-                    rhs=codes[:].bitcast(FP8X4),
-                    rhs_scale=scales[:],
-                    start=(h == 0),
-                    stop=(h == 1),
-                )
+        def gather_v(c, h):
+            gv[c, h] = held.tile([P, HALF], F32, name="gv_%d_%d" % (c, h), tag=after[c][h], align_bytes=64)
+            nc.vector.tensor_copy(gv[c, h][:], v_pool[c][:].indirect(offsets[:, 32 * h : 32 * (h + 1)]))
+
+        def group_v(c, h, bank):
+            nc.scalar.copy(out=v_grouped[c][h][:], in_=bank[:].rearrange("p t e -> p e t"))
+
+        def multiply_v(c, h):
+            quantise(v_codes[c][h][:], v_scales[c][h][:], v_grouped[c][h][:].rearrange("p e t -> p (e t)"))
+            nc.tensor.matmul_mx(
+                out=acc[c][:],
+                lhsT=w_codes[h][:].bitcast(FP8X4),
+                lhsT_scale=w_scales[h][:],
+                rhs=v_codes[c][h][:].bitcast(FP8X4),
+                rhs_scale=v_scales[c][h][:],
+                start=(h == 0),
+                stop=(h == 1),
+            )
+
+        def store(c):
             result = held.tile([P, P], F32, name="result_%d" % c)
-            nc.scalar.activation(out=result[:], in_=acc[:], func=ACT.Copy, scale=1.0 / 16.0)
+            nc.scalar.activation(out=result[:], in_=acc[c][:], func=ACT.Copy, scale=1.0 / 16.0)
             nc.sync.dma_start(out=out[0, :, P * c : P * (c + 1)], in_=result[:])
+
+        after = [["k_grouped_0", "k_grouped_1"], ["w_grouped_0", "w_grouped_1"]]
+        scores = [psum_s.tile([P, 4, NQ], F32, name="scores_%d" % h) for h in range(2)]
+        probs = [held.tile([P, 4, NQ], F32, name="probs_%d" % h) for h in range(2)]
+        w_grouped = [held.tile([P, NQ, 4], BF16, name="w_grouped_%d" % h, tag="w_grouped_%d" % h, align_bytes=64) for h in range(2)]
+        w_codes = [held.tile([P, NQ], U32, name="w_codes_%d" % h, align_bytes=64) for h in range(2)]
+        w_scales = [held.tile([P, NQ], U8, name="w_scales_%d" % h, align_bytes=64) for h in range(2)]
+        acc = [psum_s.tile([P, P], F32, name="acc_%d" % c) for c in range(2)]
+        v_grouped = []
+        v_codes = []
+        v_scales = []
+        for c in range(2):
+            v_grouped.append([held.tile([P, P, 4], BF16, name="v_grouped_%d_%d" % (c, h), align_bytes=64) for h in range(2)])
+            v_codes.append([held.tile([P, P], U32, name="v_codes_%d_%d" % (c, h), align_bytes=64) for h in range(2)])
+            v_scales.append([held.tile([P, P], U8, name="v_scales_%d_%d" % (c, h), align_bytes=64) for h in range(2)])
+
+        gather_k(0, 0, 2)
+        nc.scalar.copy(out=q_grouped[:], in_=q_raw[:].rearrange("p j q -> p q j"))
+        gather_row("ks")
+        keep_columns("ks", turn_row("ks"))
+        gather_row("kb")
+        quantise(q_codes[:], q_scales[:], q_grouped[:].rearrange("p q j -> p (q j)"))
+        keep_columns("kb", turn_row("kb"))
+        gather_k(1, 0, 2)
+        group_k(0, 0)
+        group_k(0, 1)
+        gather_row("vs")
+        keep_columns("vs", turn_row("vs"))
+        gather_k(2, 0, 2)
+        for h in range(2):
+            gather_k(3, h, h + 1)
+            group_k(1, h)
+        score(0)
+        squash(0)
+        gather_v(0, 0)
+        v00 = turn(gv[0, 0][:])
+        score(1)
+        group_v(0, 0, v00)
+        squash(1)
+        gather_v(0, 1)
+        v01 = turn(gv[0, 1][:])
+        weigh(0)
+        multiply_v(0, 0)
+        group_v(0, 1, v01)
+        weigh(1)
+        gather_v(1, 0)
+        v10 = turn(gv[1, 0][:])
+        multiply_v(0, 1)
+        gather_v(1, 1)
+        store(0)
+        group_v(1, 0, v10)
+        multiply_v(1, 0)
+        v11 = turn(gv[1, 1][:])
+        group_v(1, 1, v11)
+        multiply_v(1, 1)
+        store(1)

from contextlib import ExitStack

import concourse.mybir as mybir
from concourse.masks import make_identity

F32 = mybir.dt.float32
BF16 = mybir.dt.bfloat16
U32 = mybir.dt.uint32
U16 = mybir.dt.uint16
U8 = mybir.dt.uint8
FP8X4 = mybir.dt.float8_e4m3fn_x4
ACT = mybir.ActivationFunctionType
MULT = mybir.AluOpType.mult

P = 128
T = 4096
N = 1024
D = 512
DV = 256
NQ = 128
HALF = 512
FLOPS = 2 * N * NQ * (D + DV)
BYTES = 4 * (D * T + DV * T + D * NQ + 3 * T + NQ * DV) + 2 * P * N // 16


def tile_attend_sigmoid_ks_srt_kernel(tc, qT, kT, vT, ks, vs, kb, offs, out):
    nc = tc.nc
    with ExitStack() as ctx:
        held = ctx.enter_context(tc.tile_pool(name="held", bufs=1))
        psum_t = ctx.enter_context(tc.psum_pool(name="psum_t", bufs=4))
        psum_s = ctx.enter_context(tc.psum_pool(name="psum_s", bufs=1))

        offsets = held.tile([P, N // 16], U16, name="offsets")
        nc.sync.dma_start(offsets[:], offs)

        rows = {}
        gathered_rows = {}
        columns = {}
        for name in ("ks", "kb", "vs"):
            rows[name] = held.tile([P, T], F32, name="row_" + name)
            gathered_rows[name] = held.tile([P, N], F32, name="picked_" + name)
            columns[name] = held.tile([P, 2, 4], F32, name="col_" + name)
        k_pool = [held.tile([P, T], F32, name="k_pool_%d" % t) for t in range(4)]
        v_pool = [held.tile([P, T], F32, name="v_pool_%d" % c) for c in range(2)]
        k_rows = kT.rearrange("(p j) w -> p j w", j=4)
        q_raw = held.tile([P, 4, NQ], F32, name="q_raw")
        warm = held.tile([P, 1], F32, name="warm")
        ident = held.tile([P, P], F32, name="ident")

        nc.sync.dma_start(out=k_pool[0][:], in_=k_rows[:, 0, :])
        nc.sync.dma_start(out=q_raw[:], in_=qT[0].rearrange("(p j) q -> p j q", j=4))
        make_identity(nc, ident[:])
        nc.vector.memset(rows["ks"][:], 0.0)
        nc.sync.dma_start(out=rows["ks"][0:1, :], in_=ks[0:1, :])
        nc.vector.memset(rows["kb"][:], 0.0)
        nc.sync.dma_start(out=rows["kb"][0:1, :], in_=kb[0:1, :])
        nc.vector.memset(k_pool[1][:, 0:8], 0.0)
        nc.sync.dma_start(out=k_pool[1][:], in_=k_rows[:, 1, :])
        nc.vector.memset(rows["vs"][:], 0.0)
        nc.sync.dma_start(out=rows["vs"][0:1, :], in_=vs[0:1, :])
        nc.vector.memset(warm[:], 0.0)
        nc.scalar.activation(out=warm[:], in_=warm[:], func=ACT.Sigmoid)
        for late in (k_pool[2], k_pool[3], v_pool[0], v_pool[1]):
            nc.vector.memset(late[:, 0:8], 0.0)
        for t in range(2, 4):
            nc.sync.dma_start(out=k_pool[t][:], in_=k_rows[:, t, :])
        for c in range(2):
            nc.sync.dma_start(out=v_pool[c][:], in_=vT[P * c : P * (c + 1), :])

        gk = held.tile([P, 4, N], F32, name="gk")
        gv = {}
        k_grouped = [held.tile([P, 4, P, 4], BF16, name="k_grouped_%d" % h, tag="k_grouped_%d" % h, align_bytes=64) for h in range(2)]
        k_codes = [held.tile([P, HALF], U32, name="k_codes_%d" % h, align_bytes=64) for h in range(2)]
        k_scales = [held.tile([P, HALF], U8, name="k_scales_%d" % h, align_bytes=64) for h in range(2)]
        q_grouped = held.tile([P, NQ, 4], BF16, name="q_grouped", align_bytes=64)
        q_codes = held.tile([P, NQ], U32, name="q_codes", align_bytes=64)
        q_scales = held.tile([P, NQ], U8, name="q_scales", align_bytes=64)

        def gather_row(name):
            nc.vector.tensor_copy(gathered_rows[name][:], rows[name][:].indirect(offsets[:]))

        def turn(source):
            bank = psum_t.tile([P, 4, P], F32, name="turned")
            for t in range(4):
                nc.tensor.transpose(bank[:, t, :], source[:, t:HALF:4], ident[:])
            return bank

        def turn_row(name):
            return [turn(gathered_rows[name][:, HALF * h : HALF * (h + 1)]) for h in range(2)]

        def keep_columns(name, banks):
            for h in range(2):
                nc.scalar.copy(out=columns[name][:, h, :], in_=banks[h][:, :, 0])

        def gather_k(t, h0, h1):
            nc.vector.tensor_copy(
                gk[:, t, HALF * h0 : HALF * h1], k_pool[t][:].indirect(offsets[:, 32 * h0 : 32 * h1])
            )

        def group_k(pair, h):
            nc.scalar.copy(
                out=k_grouped[h][:, :, :, 2 * pair : 2 * pair + 2].rearrange("p t s d -> p s t d"),
                in_=gk[:, 2 * pair : 2 * pair + 2, HALF * h : HALF * (h + 1)].rearrange("p d (s t) -> p s t d", t=4),
            )

        def quantise(codes, scales, values):
            nc.vector.quantize_mx(out=codes.bitcast(FP8X4), scales=scales, in_=values)

        def score(h):
            quantise(k_codes[h][:], k_scales[h][:], k_grouped[h][:].rearrange("p t s d -> p (t s d)"))
            for t in range(4):
                nc.tensor.matmul_mx(
                    out=scores[h][:, t, :],
                    lhsT=k_codes[h][:, P * t : P * (t + 1)].bitcast(FP8X4),
                    lhsT_scale=k_scales[h][:, P * t : P * (t + 1)],
                    rhs=q_codes[:].bitcast(FP8X4),
                    rhs_scale=q_scales[:],
                    start=True,
                    stop=True,
                )

        def squash(h):
            for t in range(4):
                nc.scalar.activation(
                    out=probs[h][:, t, :],
                    in_=scores[h][:, t, :],
                    func=ACT.Sigmoid,
                    bias=columns["kb"][:, h, t : t + 1],
                    scale=columns["ks"][:, h, t : t + 1],
                )

        def weigh(h):
            nc.vector.tensor_tensor(
                w_grouped[h][:],
                probs[h][:].rearrange("p t q -> p q t"),
                columns["vs"][:, h, :].unsqueeze(1).to_broadcast([P, NQ, 4]),
                MULT,
            )
            quantise(w_codes[h][:], w_scales[h][:], w_grouped[h][:].rearrange("p q t -> p (q t)"))

        def gather_v(c, h):
            gv[c, h] = held.tile([P, HALF], F32, name="gv_%d_%d" % (c, h), tag=after[c][h], align_bytes=64)
            nc.vector.tensor_copy(gv[c, h][:], v_pool[c][:].indirect(offsets[:, 32 * h : 32 * (h + 1)]))

        def group_v(c, h, bank):
            nc.scalar.copy(out=v_grouped[c][h][:], in_=bank[:].rearrange("p t e -> p e t"))

        def multiply_v(c, h):
            quantise(v_codes[c][h][:], v_scales[c][h][:], v_grouped[c][h][:].rearrange("p e t -> p (e t)"))
            nc.tensor.matmul_mx(
                out=acc[c][:],
                lhsT=w_codes[h][:].bitcast(FP8X4),
                lhsT_scale=w_scales[h][:],
                rhs=v_codes[c][h][:].bitcast(FP8X4),
                rhs_scale=v_scales[c][h][:],
                start=(h == 0),
                stop=(h == 1),
            )

        def store(c):
            result = held.tile([P, P], F32, name="result_%d" % c)
            nc.scalar.activation(out=result[:], in_=acc[c][:], func=ACT.Copy, scale=1.0 / 16.0)
            nc.sync.dma_start(out=out[0, :, P * c : P * (c + 1)], in_=result[:])

        after = [["k_grouped_0", "k_grouped_1"], ["w_grouped_0", "w_grouped_1"]]
        scores = [psum_s.tile([P, 4, NQ], F32, name="scores_%d" % h) for h in range(2)]
        probs = [held.tile([P, 4, NQ], F32, name="probs_%d" % h) for h in range(2)]
        w_grouped = [held.tile([P, NQ, 4], BF16, name="w_grouped_%d" % h, tag="w_grouped_%d" % h, align_bytes=64) for h in range(2)]
        w_codes = [held.tile([P, NQ], U32, name="w_codes_%d" % h, align_bytes=64) for h in range(2)]
        w_scales = [held.tile([P, NQ], U8, name="w_scales_%d" % h, align_bytes=64) for h in range(2)]
        acc = [psum_s.tile([P, P], F32, name="acc_%d" % c) for c in range(2)]
        v_grouped = []
        v_codes = []
        v_scales = []
        for c in range(2):
            v_grouped.append([held.tile([P, P, 4], BF16, name="v_grouped_%d_%d" % (c, h), align_bytes=64) for h in range(2)])
            v_codes.append([held.tile([P, P], U32, name="v_codes_%d_%d" % (c, h), align_bytes=64) for h in range(2)])
            v_scales.append([held.tile([P, P], U8, name="v_scales_%d_%d" % (c, h), align_bytes=64) for h in range(2)])

        gather_k(0, 0, 2)
        nc.scalar.copy(out=q_grouped[:], in_=q_raw[:].rearrange("p j q -> p q j"))
        gather_row("ks")
        keep_columns("ks", turn_row("ks"))
        gather_row("kb")
        quantise(q_codes[:], q_scales[:], q_grouped[:].rearrange("p q j -> p (q j)"))
        keep_columns("kb", turn_row("kb"))
        gather_k(1, 0, 2)
        group_k(0, 0)
        group_k(0, 1)
        gather_row("vs")
        keep_columns("vs", turn_row("vs"))
        gather_k(2, 0, 2)
        for h in range(2):
            gather_k(3, h, h + 1)
            group_k(1, h)
        score(0)
        squash(0)
        gather_v(0, 0)
        v00 = turn(gv[0, 0][:])
        score(1)
        group_v(0, 0, v00)
        squash(1)
        gather_v(0, 1)
        v01 = turn(gv[0, 1][:])
        weigh(0)
        multiply_v(0, 0)
        group_v(0, 1, v01)
        weigh(1)
        gather_v(1, 0)
        v10 = turn(gv[1, 0][:])
        multiply_v(0, 1)
        gather_v(1, 1)
        store(0)
        group_v(1, 0, v10)
        multiply_v(1, 0)
        v11 = turn(gv[1, 1][:])
        group_v(1, 1, v11)
        multiply_v(1, 1)
        store(1)
